import numpy as np
import ml_dtypes


def mxq(x, axis, fmt="e4m3"):
    dtype, down = {"e4m3": (ml_dtypes.float8_e4m3fn, 7), "e5m2": (ml_dtypes.float8_e5m2, 14)}[fmt]
    v = np.moveaxis(np.asarray(x, np.float32).astype(ml_dtypes.bfloat16).astype(np.float64), axis, -1)
    blocks = v.reshape(v.shape[:-1] + (-1, 32))
    amax = np.abs(blocks).max(-1, keepdims=True)
    byte = np.maximum(np.where(amax > 0, np.frexp(amax)[1] - 1 + 127, 0) - down, 1)
    scale = np.exp2(byte - 127.0)
    codes = (blocks / scale).astype(np.float32).astype(dtype).astype(np.float64)
    return np.moveaxis((codes * scale).reshape(v.shape), -1, axis)


WIDE = False


def mx_kscale(k):
    if not WIDE:
        return np.ones(k)
    levels = np.array([10, -10, 5, -5, 0])
    if k % 512:
        return np.exp2(np.random.permutation(np.resize(levels, k // 32))).repeat(32)
    a = np.empty((k // 512, 16))
    for p in range(k // 512):
        a[p, :8] = np.random.permutation(np.resize(levels, 8))
        for g in range(8):
            far = levels[np.abs(levels - a[p, g]) >= 10]
            a[p, g + 8] = far[np.random.randint(len(far))]
    return np.exp2(a.ravel()).repeat(32)


def f64(x):
    return np.asarray(x).astype(np.float64)


def striped(idx):
    return np.tile(idx.reshape(-1, 16).T, (8, 1)).astype(np.uint16)


def unstriped(offs):
    return offs[:16].T.reshape(-1).astype(np.int64)


def pack_weight(w):
    k, n = w.shape
    w = f64(np.asarray(w, np.float32).astype(ml_dtypes.bfloat16)).reshape(k // 32, 32, n)
    amax = np.abs(w).max(1)
    byte = np.clip(np.where(amax > 0, np.frexp(amax)[1] - 1 + 127 - 7, 1), 1, 254)
    scaled = (w * np.exp2(127.0 - byte)[:, None, :]).reshape(k, n).astype(np.float32)
    words = np.ascontiguousarray(scaled.reshape(k // 512, 128, 4, n).transpose(0, 1, 3, 2)).astype(ml_dtypes.float8_e4m3fn).view(np.uint8)
    return words, np.ascontiguousarray(byte.astype(np.uint8).reshape(k // 512, 16, n))


def unpack_weight(words, scales):
    g, p, n, _ = words.shape
    vals = np.ascontiguousarray(words).view(ml_dtypes.float8_e4m3fn).astype(np.float64) * np.repeat(np.exp2(scales.astype(np.float64) - 127.0), 8, axis=1)[..., None]
    return vals.transpose(0, 1, 3, 2).reshape(g * 512, n)


K, T, S, V, H, N = 512, 2048, 1536, 512, 512, 256


def setup_inputs():
    n = np.random.standard_normal
    s = mx_kscale(K)[:, None]
    u = mx_kscale(H)
    packed_xT = pack_weight(n((K, T)) * s)
    return {
        "x_words": packed_xT[0],
        "x_scales": packed_xT[1],
        "w1": (n((K, H)) / np.sqrt(K) / s * u).astype(np.float32),
        "w2": (n((K, H)) / np.sqrt(K) / s).astype(np.float32),
        "w3": (n((K, H)) / np.sqrt(K) / s).astype(np.float32),
        "w4": (n((H, N)) / np.sqrt(H) / u[:, None]).astype(np.float32),
        "offs": striped(np.random.permutation(T)[:S]),
    }


def reference(x_words, x_scales, w1, w2, w3, w4, offs):
    xq = unpack_weight(x_words, x_scales)[:, unstriped(offs)]
    z = (((mxq(f64(w1), 0, "e4m3").T @ xq[:, :V])) * ((mxq(f64(w2), 0, "e4m3").T @ xq[:, V:2 * V]))) * ((mxq(f64(w3), 0, "e4m3").T @ xq[:, 2 * V:3 * V]))
    return mxq(f64(w4), 0, "e4m3").T @ mxq(z, 0, "e4m3")

@@ -1,0 +1,151 @@
+from contextlib import ExitStack
+
+import concourse.mybir as mybir
+
+K, T, S, V, H, N = 512, 2048, 1536, 512, 512, 256
+FLOPS = 2 * (3 * K * H * V + H * N * V)
+
+F32 = mybir.dt.float32
+BF16 = mybir.dt.bfloat16
+I32 = mybir.dt.int32
+U32 = mybir.dt.uint32
+U16 = mybir.dt.uint16
+U8 = mybir.dt.uint8
+FP8X4 = mybir.dt.float8_e4m3fn_x4
+MULT = mybir.AluOpType.mult
+
+P = 128
+PACK = 4
+CHUNK = 128
+CHUNKS = V // CHUNK
+
+
+def tile_picked_trilin_none_p_kernel(tc, x_words, x_scales, w1, w2, w3, w4, offs, out):
+    nc = tc.nc
+    with ExitStack() as ctx:
+        keep = ctx.enter_context(tc.tile_pool(name="keep", bufs=1))
+        psum = ctx.enter_context(tc.psum_pool(name="psum", bufs=CHUNKS))
+
+        offsets = keep.tile([P, S // 16], U16, name="offsets")
+        nc.sync.dma_start(offsets[:], offs)
+
+        scale_table = keep.tile([P, T], U8, name="scale_table", align_bytes=64)
+        nc.vector.memset(scale_table[:].bitcast(I32), 0)
+
+        def rows_of(w):
+            return w.rearrange("(p j) c -> p j c", j=PACK)
+
+        def load_weight(w, name):
+            raw = keep.tile([P, PACK, w.shape[1]], F32, name=name, tag=name, align_bytes=64)
+            nc.sync.dma_start(raw[:], rows_of(w))
+            return raw
+
+        raw1 = keep.tile([P, PACK, H], F32, name="raw1", align_bytes=64)
+        nc.sync.dma_start(raw1[:, 0:1, :], rows_of(w1)[:, 0:1, :])
+        for q in range(4):
+            nc.sync.dma_start(scale_table[32 * q : 32 * q + 4, :].bitcast(I32), x_scales[0, 4 * q : 4 * q + 4, :].bitcast(I32))
+        nc.sync.dma_start(raw1[:, 1:PACK, :], rows_of(w1)[:, 1:PACK, :])
+        word_table = keep.tile([P, T], U32, name="word_table", align_bytes=64)
+        nc.sync.dma_start(word_table[:].bitcast(I32), x_words[0].rearrange("p n j -> p (n j)").bitcast(I32))
+        raw2 = load_weight(w2, "raw2")
+        raw3 = load_weight(w3, "raw3")
+        raw4 = load_weight(w4, "raw4")
+
+        def quantize(grouped, name):
+            width = grouped.shape[1] // PACK
+            codes = keep.tile([P, width], U32, name=name + "_codes", align_bytes=64)
+            scales = keep.tile([P, width], U8, name=name + "_scales", align_bytes=64)
+            nc.vector.quantize_mx(out=codes[:].bitcast(FP8X4), scales=scales[:], in_=grouped[:])
+            return codes, scales
+
+        def round_first_weight(raw, half, copy, name):
+            grouped = keep.tile([P, H * PACK // 2], BF16, name=name, tag=name, align_bytes=64)
+            copy(
+                grouped[:].rearrange("p (t m j) -> p m j t", t=2, j=PACK),
+                raw[:].rearrange("p j (m t) -> p m j t", t=PACK)[:, :, :, 2 * half : 2 * half + 2],
+            )
+            return grouped
+
+        def gather_words(d, tag):
+            words = keep.tile([P, V], U32, name=f"x_picked{d}", tag=tag, align_bytes=64)
+            nc.vector.tensor_copy(words[:], word_table[:].indirect(offsets[:, d * V // 16 : (d + 1) * V // 16]))
+            return words
+
+        def first_product(weight, words, d, c, tag):
+            bank = psum.tile([P, PACK, CHUNK], F32, name=f"prod{d}_{c}", tag=tag)
+            for t in range(PACK):
+                codes, scales = weight[t // 2]
+                m_cols = slice(t % 2 * P, (t % 2 + 1) * P)
+                nc.tensor.matmul_mx(
+                    out=bank[:, t, :],
+                    lhsT=codes[:, m_cols].bitcast(FP8X4),
+                    lhsT_scale=scales[:, m_cols],
+                    rhs=words[:, c * CHUNK : (c + 1) * CHUNK].bitcast(FP8X4),
+                    rhs_scale=picked_scales[:, d * V + c * CHUNK : d * V + (c + 1) * CHUNK],
+                    start=True,
+                    stop=True,
+                )
+            return bank[:].rearrange("p t v -> p v t")
+
+        picked_scales = keep.tile([P, S], U8, name="picked_scales", align_bytes=64)
+        nc.vector.tensor_copy(picked_scales[:], scale_table[:].indirect(offsets[:]))
+
+        on_scalar, on_vector = nc.scalar.copy, nc.vector.tensor_copy
+        g1 = [round_first_weight(raw1, half, on_scalar, f"g1{half}") for half in range(2)]
+        x1 = gather_words(0, "x1")
+        q1 = [quantize(g1[half], f"w1{half}") for half in range(2)]
+        x2 = gather_words(1, "g11")
+        g2 = [round_first_weight(raw2, 0, on_scalar, "g20"), round_first_weight(raw2, 1, on_vector, "g21")]
+        q2 = [quantize(g2[half], f"w2{half}") for half in range(2)]
+        x3 = gather_words(2, "g21")
+
+        a_all = keep.tile([P, CHUNKS * CHUNK * PACK], F32, name="a_all", tag="raw2", align_bytes=64)
+        a_sb = [a_all[:, c * CHUNK * PACK : (c + 1) * CHUNK * PACK].rearrange("p (v t) -> p v t", t=PACK) for c in range(CHUNKS)]
+        for c in range(CHUNKS):
+            nc.scalar.copy(a_sb[c], first_product(q1, x1, 0, c, "ac"))
+
+        def make_ab(c, tag):
+            b_bank = first_product(q2, x2, 1, c, "bo")
+            ab_tile = keep.tile([P, CHUNK, PACK], F32, name=f"ab{c}", tag=tag, align_bytes=64)
+            nc.vector.tensor_tensor(ab_tile[:], b_bank, a_sb[c], MULT)
+            return ab_tile
+
+        ab_sb = [make_ab(c, f"ab{c}") for c in range(CHUNKS - 1)]
+        q3 = [quantize(round_first_weight(raw3, half, on_scalar, f"g3{half}"), f"w3{half}") for half in range(2)]
+        ab_sb.append(make_ab(CHUNKS - 1, "g31"))
+        g4 = keep.tile([P, N * PACK], BF16, name="g4", align_bytes=64)
+        nc.scalar.copy(
+            g4[:].rearrange("p (c i j) -> p c j i", i=4, j=PACK),
+            raw4[:].rearrange("p j (c i) -> p c j i", i=4),
+        )
+        w4_codes, w4_scales = quantize(g4, "w4")
+
+        def make_z(c):
+            c_bank = first_product(q3, x3, 2, c, "ac")
+            z = keep.tile([P, CHUNK * PACK], BF16, name=f"z{c}", align_bytes=64)
+            nc.vector.tensor_tensor(z[:].rearrange("p (v t) -> p v t", t=PACK), c_bank, ab_sb[c][:], MULT)
+            return z
+
+        def finish(c, z):
+            z_codes, z_scales = quantize(z, f"z{c}")
+            bank = psum.tile([P, N // P, CHUNK], F32, name=f"o{c}", tag="bo")
+            for h in range(N // P):
+                m_cols = slice(h * P, (h + 1) * P)
+                nc.tensor.matmul_mx(
+                    out=bank[:, h, :],
+                    lhsT=w4_codes[:, m_cols].bitcast(FP8X4),
+                    lhsT_scale=w4_scales[:, m_cols],
+                    rhs=z_codes[:].bitcast(FP8X4),
+                    rhs_scale=z_scales[:],
+                    start=True,
+                    stop=True,
+                )
+            result = keep.tile([P, N // P, CHUNK], F32, name=f"result{c}")
+            nc.scalar.copy(result[:], bank[:])
+            nc.sync.dma_start(out.rearrange("(h m) v -> m h v", m=P)[:, :, c * CHUNK : (c + 1) * CHUNK], result[:])
+
+        zs = [make_z(0)]
+        for c in range(1, CHUNKS):
+            zs.append(make_z(c))
+            finish(c - 1, zs[c - 1])
+        finish(CHUNKS - 1, zs[-1])

@@ -42,8 +42,9 @@ def tile_picked_trilin_none_p_kernel(tc, x_words, x_scales, w1, w2, w3, w4, offs
 
         raw1 = keep.tile([P, PACK, H], F32, name="raw1", align_bytes=64)
         nc.sync.dma_start(raw1[:, 0:1, :], rows_of(w1)[:, 0:1, :])
-        for q in range(4):
-            nc.sync.dma_start(scale_table[32 * q : 32 * q + 4, :].bitcast(I32), x_scales[0, 4 * q : 4 * q + 4, :].bitcast(I32))
+        scale_rows = x_scales[0].bitcast(I32).rearrange("(q r) c -> r q c", r=4)
+        for r in range(4):
+            nc.sync.dma_start(scale_table[r:P:32, :].bitcast(I32), scale_rows[r])
         nc.sync.dma_start(raw1[:, 1:PACK, :], rows_of(w1)[:, 1:PACK, :])
         word_table = keep.tile([P, T], U32, name="word_table", align_bytes=64)
         nc.sync.dma_start(word_table[:].bitcast(I32), x_words[0].rearrange("p n j -> p (n j)").bitcast(I32))
@@ -85,7 +86,7 @@ def tile_picked_trilin_none_p_kernel(tc, x_words, x_scales, w1, w2, w3, w4, offs
                     start=True,
                     stop=True,
                 )
-            return bank[:].rearrange("p t v -> p v t")
+            return bank[:].rearrange("p t (v e) -> p v t e", e=2)
 
         picked_scales = keep.tile([P, S], U8, name="picked_scales", align_bytes=64)
         nc.vector.tensor_copy(picked_scales[:], scale_table[:].indirect(offsets[:]))
@@ -100,13 +101,13 @@ def tile_picked_trilin_none_p_kernel(tc, x_words, x_scales, w1, w2, w3, w4, offs
         x3 = gather_words(2, "g21")
 
         a_all = keep.tile([P, CHUNKS * CHUNK * PACK], F32, name="a_all", tag="raw2", align_bytes=64)
-        a_sb = [a_all[:, c * CHUNK * PACK : (c + 1) * CHUNK * PACK].rearrange("p (v t) -> p v t", t=PACK) for c in range(CHUNKS)]
+        a_sb = [a_all[:, c * CHUNK * PACK : (c + 1) * CHUNK * PACK].rearrange("p (v t e) -> p v t e", t=PACK, e=2) for c in range(CHUNKS)]
         for c in range(CHUNKS):
             nc.scalar.copy(a_sb[c], first_product(q1, x1, 0, c, "ac"))
 
         def make_ab(c, tag):
             b_bank = first_product(q2, x2, 1, c, "bo")
-            ab_tile = keep.tile([P, CHUNK, PACK], F32, name=f"ab{c}", tag=tag, align_bytes=64)
+            ab_tile = keep.tile([P, CHUNK // 2, PACK, 2], F32, name=f"ab{c}", tag=tag, align_bytes=64)
             nc.vector.tensor_tensor(ab_tile[:], b_bank, a_sb[c], MULT)
             return ab_tile
 
@@ -123,7 +124,7 @@ def tile_picked_trilin_none_p_kernel(tc, x_words, x_scales, w1, w2, w3, w4, offs
         def make_z(c):
             c_bank = first_product(q3, x3, 2, c, "ac")
             z = keep.tile([P, CHUNK * PACK], BF16, name=f"z{c}", align_bytes=64)
-            nc.vector.tensor_tensor(z[:].rearrange("p (v t) -> p v t", t=PACK), c_bank, ab_sb[c][:], MULT)
+            nc.vector.tensor_tensor(z[:].rearrange("p (v e t) -> p v t e", t=PACK, e=2), c_bank, ab_sb[c][:], MULT)
             return z
 
         def finish(c, z):

@@ -40,14 +40,14 @@ def tile_picked_trilin_none_p_kernel(tc, x_words, x_scales, w1, w2, w3, w4, offs
             nc.sync.dma_start(raw[:], rows_of(w))
             return raw
 
-        raw1 = keep.tile([P, PACK, H], F32, name="raw1", align_bytes=64)
-        nc.sync.dma_start(raw1[:, 0:1, :], rows_of(w1)[:, 0:1, :])
+        word_table = keep.tile([P, T], U32, name="word_table", align_bytes=64)
+        word_rows = x_words[0].rearrange("p n j -> p (n j)").bitcast(I32)
+        nc.sync.dma_start(word_table[:, :512].bitcast(I32), word_rows[:, :512])
         scale_rows = x_scales[0].bitcast(I32).rearrange("(q r) c -> r q c", r=4)
         for r in range(4):
             nc.sync.dma_start(scale_table[r:P:32, :].bitcast(I32), scale_rows[r])
-        nc.sync.dma_start(raw1[:, 1:PACK, :], rows_of(w1)[:, 1:PACK, :])
-        word_table = keep.tile([P, T], U32, name="word_table", align_bytes=64)
-        nc.sync.dma_start(word_table[:].bitcast(I32), x_words[0].rearrange("p n j -> p (n j)").bitcast(I32))
+        nc.sync.dma_start(word_table[:, 512:].bitcast(I32), word_rows[:, 512:])
+        raw1 = load_weight(w1, "raw1")
         raw2 = load_weight(w2, "raw2")
         raw3 = load_weight(w3, "raw3")
         raw4 = load_weight(w4, "raw4")
@@ -59,8 +59,8 @@ def tile_picked_trilin_none_p_kernel(tc, x_words, x_scales, w1, w2, w3, w4, offs
             nc.vector.quantize_mx(out=codes[:].bitcast(FP8X4), scales=scales[:], in_=grouped[:])
             return codes, scales
 
-        def round_first_weight(raw, half, copy, name):
-            grouped = keep.tile([P, H * PACK // 2], BF16, name=name, tag=name, align_bytes=64)
+        def round_first_weight(raw, half, copy, name, tag):
+            grouped = keep.tile([P, H * PACK // 2], BF16, name=name, tag=tag, align_bytes=64)
             copy(
                 grouped[:].rearrange("p (t m j) -> p m j t", t=2, j=PACK),
                 raw[:].rearrange("p j (m t) -> p m j t", t=PACK)[:, :, :, 2 * half : 2 * half + 2],
@@ -92,15 +92,24 @@ def tile_picked_trilin_none_p_kernel(tc, x_words, x_scales, w1, w2, w3, w4, offs
         nc.vector.tensor_copy(picked_scales[:], scale_table[:].indirect(offsets[:]))
 
         on_scalar, on_vector = nc.scalar.copy, nc.vector.tensor_copy
-        g1 = [round_first_weight(raw1, half, on_scalar, f"g1{half}") for half in range(2)]
-        x1 = gather_words(0, "x1")
-        q1 = [quantize(g1[half], f"w1{half}") for half in range(2)]
-        x2 = gather_words(1, "g11")
-        g2 = [round_first_weight(raw2, 0, on_scalar, "g20"), round_first_weight(raw2, 1, on_vector, "g21")]
-        q2 = [quantize(g2[half], f"w2{half}") for half in range(2)]
-        x3 = gather_words(2, "g21")
 
-        a_all = keep.tile([P, CHUNKS * CHUNK * PACK], F32, name="a_all", tag="raw2", align_bytes=64)
+        def on_gpsimd(target, source):
+            nc.gpsimd.tensor_scalar(target, source, 1.0, 0.0, MULT, mybir.AluOpType.add)
+
+        x1 = gather_words(0, "x1")
+        x2 = gather_words(1, "x2")
+        g1 = keep.tile([P, H * PACK], BF16, name="g1", tag="g1", align_bytes=64)
+        for half in range(2):
+            on_scalar(
+                g1[:, half * 1024 : (half + 1) * 1024].rearrange("p (t m j) -> p m j t", t=2, j=PACK),
+                raw1[:].rearrange("p j (m t) -> p m j t", t=PACK)[:, :, :, 2 * half : 2 * half + 2],
+            )
+        w1_codes, w1_scales = quantize(g1, "w1")
+        q1 = [(w1_codes[:, 256 * half : 256 * (half + 1)], w1_scales[:, 256 * half : 256 * (half + 1)]) for half in range(2)]
+        x3 = gather_words(2, "g1")
+        q2 = [quantize(round_first_weight(raw2, half, on_scalar, f"g2{half}", f"g2{half}"), f"w2{half}") for half in range(2)]
+
+        a_all = keep.tile([P, CHUNKS * CHUNK * PACK], F32, name="a_all", align_bytes=64)
         a_sb = [a_all[:, c * CHUNK * PACK : (c + 1) * CHUNK * PACK].rearrange("p (v t e) -> p v t e", t=PACK, e=2) for c in range(CHUNKS)]
         for c in range(CHUNKS):
             nc.scalar.copy(a_sb[c], first_product(q1, x1, 0, c, "ac"))
@@ -112,8 +121,15 @@ def tile_picked_trilin_none_p_kernel(tc, x_words, x_scales, w1, w2, w3, w4, offs
             return ab_tile
 
         ab_sb = [make_ab(c, f"ab{c}") for c in range(CHUNKS - 1)]
-        q3 = [quantize(round_first_weight(raw3, half, on_scalar, f"g3{half}"), f"w3{half}") for half in range(2)]
-        ab_sb.append(make_ab(CHUNKS - 1, "g31"))
+        g31 = keep.tile([P, H * PACK // 2], BF16, name="g31", tag="g21", align_bytes=64)
+        on_gpsimd(
+            g31[:].rearrange("p (t m j) -> p t m j", t=2, j=PACK),
+            raw3[:].rearrange("p j (m t) -> p t m j", t=PACK)[:, 2:4],
+        )
+        w3_high = quantize(g31, "w31")
+        w3_low = quantize(round_first_weight(raw3, 0, on_scalar, "g30", "g30"), "w30")
+        q3 = [w3_low, w3_high]
+        ab_sb.append(make_ab(CHUNKS - 1, "g30"))
         g4 = keep.tile([P, N * PACK], BF16, name="g4", align_bytes=64)
         nc.scalar.copy(
             g4[:].rearrange("p (c i j) -> p c j i", i=4, j=PACK),
@@ -121,32 +137,47 @@ def tile_picked_trilin_none_p_kernel(tc, x_words, x_scales, w1, w2, w3, w4, offs
         )
         w4_codes, w4_scales = quantize(g4, "w4")
 
+        z_first = keep.tile([P, 2 * CHUNK * PACK], BF16, name="z_first", align_bytes=64)
+        z_third = keep.tile([P, CHUNK * PACK], BF16, name="z_third", align_bytes=64)
+        z_last = keep.tile([P, CHUNK * PACK], BF16, name="z_last", align_bytes=64)
+        z_of = [z_first[:, : CHUNK * PACK], z_first[:, CHUNK * PACK :], z_third[:], z_last[:]]
+
         def make_z(c):
             c_bank = first_product(q3, x3, 2, c, "ac")
-            z = keep.tile([P, CHUNK * PACK], BF16, name=f"z{c}", align_bytes=64)
-            nc.vector.tensor_tensor(z[:].rearrange("p (v e t) -> p v t e", t=PACK, e=2), c_bank, ab_sb[c][:], MULT)
-            return z
+            nc.vector.tensor_tensor(z_of[c].rearrange("p (v e t) -> p v t e", t=PACK, e=2), c_bank, ab_sb[c][:], MULT)
 
-        def finish(c, z):
-            z_codes, z_scales = quantize(z, f"z{c}")
-            bank = psum.tile([P, N // P, CHUNK], F32, name=f"o{c}", tag="bo")
-            for h in range(N // P):
-                m_cols = slice(h * P, (h + 1) * P)
-                nc.tensor.matmul_mx(
-                    out=bank[:, h, :],
-                    lhsT=w4_codes[:, m_cols].bitcast(FP8X4),
-                    lhsT_scale=w4_scales[:, m_cols],
-                    rhs=z_codes[:].bitcast(FP8X4),
-                    rhs_scale=z_scales[:],
-                    start=True,
-                    stop=True,
-                )
-            result = keep.tile([P, N // P, CHUNK], F32, name=f"result{c}")
-            nc.scalar.copy(result[:], bank[:])
-            nc.sync.dma_start(out.rearrange("(h m) v -> m h v", m=P)[:, :, c * CHUNK : (c + 1) * CHUNK], result[:])
+        def second_product(z_codes, z_scales, h, target):
+            m_cols = slice(h * P, (h + 1) * P)
+            nc.tensor.matmul_mx(
+                out=target,
+                lhsT=w4_codes[:, m_cols].bitcast(FP8X4),
+                lhsT_scale=w4_scales[:, m_cols],
+                rhs=z_codes[:].bitcast(FP8X4),
+                rhs_scale=z_scales[:],
+                start=True,
+                stop=True,
+            )
 
-        zs = [make_z(0)]
-        for c in range(1, CHUNKS):
-            zs.append(make_z(c))
-            finish(c - 1, zs[c - 1])
-        finish(CHUNKS - 1, zs[-1])
+        def finish(first, z, split):
+            width = z.shape[1] // PACK
+            z_codes, z_scales = quantize(z, f"z{first}")
+            result = keep.tile([P, N // P, width], F32, name=f"result{first}")
+            if split:
+                for h, copy in enumerate((on_scalar, on_vector)):
+                    bank = psum.tile([P, width], F32, name=f"o{first}_{h}", tag="bo")
+                    second_product(z_codes, z_scales, h, bank[:])
+                    copy(result[:, h, :], bank[:])
+            else:
+                bank = psum.tile([P, N // P, width], F32, name=f"o{first}", tag="bo")
+                for h in range(N // P):
+                    second_product(z_codes, z_scales, h, bank[:, h, :])
+                on_scalar(result[:], bank[:])
+            nc.sync.dma_start(out.rearrange("(h m) v -> m h v", m=P)[:, :, first : first + width], result[:])
+
+        make_z(0)
+        make_z(1)
+        make_z(2)
+        finish(0, z_first, False)
+        make_z(3)
+        finish(2 * CHUNK, z_third, False)
+        finish(3 * CHUNK, z_last, True)

@@ -13,11 +13,16 @@ U16 = mybir.dt.uint16
 U8 = mybir.dt.uint8
 FP8X4 = mybir.dt.float8_e4m3fn_x4
 MULT = mybir.AluOpType.mult
+ADD = mybir.AluOpType.add
 
 P = 128
 PACK = 4
+QUADRANT = 32
+STRIPE = 16
 CHUNK = 128
 CHUNKS = V // CHUNK
+PAIR = 2
+ALIGN = 64
 
 
 def tile_picked_trilin_none_p_kernel(tc, x_words, x_scales, w1, w2, w3, w4, offs, out):
@@ -26,127 +31,136 @@ def tile_picked_trilin_none_p_kernel(tc, x_words, x_scales, w1, w2, w3, w4, offs
         keep = ctx.enter_context(tc.tile_pool(name="keep", bufs=1))
         psum = ctx.enter_context(tc.psum_pool(name="psum", bufs=CHUNKS))
 
-        offsets = keep.tile([P, S // 16], U16, name="offsets")
+        offsets = keep.tile([P, S // STRIPE], U16, name="offsets")
         nc.sync.dma_start(offsets[:], offs)
 
-        scale_table = keep.tile([P, T], U8, name="scale_table", align_bytes=64)
+        scale_table = keep.tile([P, T], U8, name="scale_table", align_bytes=ALIGN)
         nc.vector.memset(scale_table[:].bitcast(I32), 0)
 
         def rows_of(w):
             return w.rearrange("(p j) c -> p j c", j=PACK)
 
         def load_weight(w, name):
-            raw = keep.tile([P, PACK, w.shape[1]], F32, name=name, tag=name, align_bytes=64)
+            raw = keep.tile([P, PACK, w.shape[1]], F32, name=name, tag=name, align_bytes=ALIGN)
             nc.sync.dma_start(raw[:], rows_of(w))
             return raw
 
-        word_table = keep.tile([P, T], U32, name="word_table", align_bytes=64)
-        word_rows = x_words[0].rearrange("p n j -> p (n j)").bitcast(I32)
-        nc.sync.dma_start(word_table[:, :512].bitcast(I32), word_rows[:, :512])
-        scale_rows = x_scales[0].bitcast(I32).rearrange("(q r) c -> r q c", r=4)
-        for r in range(4):
-            nc.sync.dma_start(scale_table[r:P:32, :].bitcast(I32), scale_rows[r])
-        nc.sync.dma_start(word_table[:, 512:].bitcast(I32), word_rows[:, 512:])
-        raw1 = load_weight(w1, "raw1")
-        raw2 = load_weight(w2, "raw2")
+        raw1 = keep.tile([P, PACK, H], F32, name="raw1", align_bytes=ALIGN)
+        nc.sync.dma_start(raw1[:, 0:1, :], rows_of(w1)[:, 0:1, :])
+        scale_rows = x_scales[0].bitcast(I32).rearrange("(q r) c -> r q c", r=PACK)
+        for r in range(PACK):
+            nc.sync.dma_start(scale_table[r:P:QUADRANT, :].bitcast(I32), scale_rows[r])
+        nc.sync.dma_start(raw1[:, 1:PACK, :], rows_of(w1)[:, 1:PACK, :])
+        word_table = keep.tile([P, T], U32, name="word_table", tag="word_table", align_bytes=ALIGN)
+        nc.sync.dma_start(word_table[:].bitcast(I32), x_words[0].rearrange("p n j -> p (n j)").bitcast(I32))
+        raw2 = []
+        for side in range(2):
+            raw = keep.tile([P, PACK, H // 2], F32, name=f"raw2_{side}", tag=f"raw2_{side}", align_bytes=ALIGN)
+            nc.sync.dma_start(raw[:], rows_of(w2)[:, :, side * H // 2 : (side + 1) * H // 2])
+            raw2.append(raw)
         raw3 = load_weight(w3, "raw3")
         raw4 = load_weight(w4, "raw4")
 
-        def quantize(grouped, name):
-            width = grouped.shape[1] // PACK
-            codes = keep.tile([P, width], U32, name=name + "_codes", align_bytes=64)
-            scales = keep.tile([P, width], U8, name=name + "_scales", align_bytes=64)
-            nc.vector.quantize_mx(out=codes[:].bitcast(FP8X4), scales=scales[:], in_=grouped[:])
+        def quantize(rounded, name):
+            width = rounded.shape[1] // PACK
+            codes = keep.tile([P, width], U32, name=name + "_codes", align_bytes=ALIGN)
+            scales = keep.tile([P, width], U8, name=name + "_scales", align_bytes=ALIGN)
+            nc.vector.quantize_mx(out=codes[:].bitcast(FP8X4), scales=scales[:], in_=rounded[:])
             return codes, scales
 
-        def round_first_weight(raw, half, copy, name, tag):
-            grouped = keep.tile([P, H * PACK // 2], BF16, name=name, tag=tag, align_bytes=64)
-            copy(
-                grouped[:].rearrange("p (t m j) -> p m j t", t=2, j=PACK),
-                raw[:].rearrange("p j (m t) -> p m j t", t=PACK)[:, :, :, 2 * half : 2 * half + 2],
+        def rounded_half(name, tag):
+            return keep.tile([P, PAIR * P * PACK], BF16, name=name, tag=tag, align_bytes=ALIGN)
+
+        def round_on_scalar(rounded, raw, half, first_m):
+            count = raw.shape[2] // PACK
+            nc.scalar.copy(
+                rounded[:].rearrange("p (t m j) -> p m j t", t=PAIR, j=PACK)[:, first_m : first_m + count],
+                raw[:].rearrange("p j (m t) -> p m j t", t=PACK)[:, :, :, PAIR * half : PAIR * (half + 1)],
             )
-            return grouped
 
-        def gather_words(d, tag):
-            words = keep.tile([P, V], U32, name=f"x_picked{d}", tag=tag, align_bytes=64)
-            nc.vector.tensor_copy(words[:], word_table[:].indirect(offsets[:, d * V // 16 : (d + 1) * V // 16]))
-            return words
+        def gather_words(first, count, tag):
+            words = keep.tile([P, count], U32, name=f"picked_words{first}", tag=tag, align_bytes=ALIGN)
+            entries = offsets[:, first // STRIPE : (first + count) // STRIPE]
+            nc.vector.tensor_copy(words[:], word_table[:].indirect(entries))
+            return [words[:, c * CHUNK : (c + 1) * CHUNK] for c in range(count // CHUNK)]
 
-        def first_product(weight, words, d, c, tag):
-            bank = psum.tile([P, PACK, CHUNK], F32, name=f"prod{d}_{c}", tag=tag)
+        def first_product(halves, words, piece, c, tag):
+            bank = psum.tile([P, PACK, CHUNK], F32, name=f"product{piece}_{c}", tag=tag)
+            entry = piece * V + c * CHUNK
             for t in range(PACK):
-                codes, scales = weight[t // 2]
-                m_cols = slice(t % 2 * P, (t % 2 + 1) * P)
+                codes, scales = halves[t // PAIR]
+                m_cols = slice(t % PAIR * P, (t % PAIR + 1) * P)
                 nc.tensor.matmul_mx(
                     out=bank[:, t, :],
                     lhsT=codes[:, m_cols].bitcast(FP8X4),
                     lhsT_scale=scales[:, m_cols],
-                    rhs=words[:, c * CHUNK : (c + 1) * CHUNK].bitcast(FP8X4),
-                    rhs_scale=picked_scales[:, d * V + c * CHUNK : d * V + (c + 1) * CHUNK],
+                    rhs=words[c].bitcast(FP8X4),
+                    rhs_scale=picked_scales[:, entry : entry + CHUNK],
                     start=True,
                     stop=True,
                 )
             return bank[:].rearrange("p t (v e) -> p v t e", e=2)
 
-        picked_scales = keep.tile([P, S], U8, name="picked_scales", align_bytes=64)
+        picked_scales = keep.tile([P, S], U8, name="picked_scales", align_bytes=ALIGN)
         nc.vector.tensor_copy(picked_scales[:], scale_table[:].indirect(offsets[:]))
 
-        on_scalar, on_vector = nc.scalar.copy, nc.vector.tensor_copy
-
-        def on_gpsimd(target, source):
-            nc.gpsimd.tensor_scalar(target, source, 1.0, 0.0, MULT, mybir.AluOpType.add)
-
-        x1 = gather_words(0, "x1")
-        x2 = gather_words(1, "x2")
-        g1 = keep.tile([P, H * PACK], BF16, name="g1", tag="g1", align_bytes=64)
+        rounded1 = [rounded_half(f"rounded1_{half}", f"rounded1_{half}") for half in range(2)]
         for half in range(2):
-            on_scalar(
-                g1[:, half * 1024 : (half + 1) * 1024].rearrange("p (t m j) -> p m j t", t=2, j=PACK),
-                raw1[:].rearrange("p j (m t) -> p m j t", t=PACK)[:, :, :, 2 * half : 2 * half + 2],
-            )
-        w1_codes, w1_scales = quantize(g1, "w1")
-        q1 = [(w1_codes[:, 256 * half : 256 * (half + 1)], w1_scales[:, 256 * half : 256 * (half + 1)]) for half in range(2)]
-        x3 = gather_words(2, "g1")
-        q2 = [quantize(round_first_weight(raw2, half, on_scalar, f"g2{half}", f"g2{half}"), f"w2{half}") for half in range(2)]
+            round_on_scalar(rounded1[half], raw1, half, 0)
+        words1 = gather_words(0, V, "words1")
+        w1_mx = [quantize(rounded1[half], f"w1_{half}") for half in range(2)]
+        words_mid = gather_words(V, V + V // 2, "rounded1_1")
+        rounded2 = [rounded_half(f"rounded2_{half}", f"rounded2_{half}") for half in range(2)]
+        for side in range(2):
+            for half in range(2):
+                round_on_scalar(rounded2[half], raw2[side], half, side * P // 2)
+        w2_mx = [quantize(rounded2[half], f"w2_{half}") for half in range(2)]
+        words2 = words_mid[:CHUNKS]
+        words3 = words_mid[CHUNKS:] + gather_words(S - V // 2, V // 2, "rounded2_1")
 
-        a_all = keep.tile([P, CHUNKS * CHUNK * PACK], F32, name="a_all", align_bytes=64)
-        a_sb = [a_all[:, c * CHUNK * PACK : (c + 1) * CHUNK * PACK].rearrange("p (v t e) -> p v t e", t=PACK, e=2) for c in range(CHUNKS)]
+        width = CHUNK * PACK
+        a_all = keep.tile([P, CHUNKS * width], F32, name="a_all", tag="raw2_1", align_bytes=ALIGN)
+        a_of = [a_all[:, c * width : (c + 1) * width].rearrange("p (v t e) -> p v t e", t=PACK, e=2) for c in range(CHUNKS)]
         for c in range(CHUNKS):
-            nc.scalar.copy(a_sb[c], first_product(q1, x1, 0, c, "ac"))
+            nc.scalar.copy(a_of[c], first_product(w1_mx, words1, 0, c, "first_third"))
 
         def make_ab(c, tag):
-            b_bank = first_product(q2, x2, 1, c, "bo")
-            ab_tile = keep.tile([P, CHUNK // 2, PACK, 2], F32, name=f"ab{c}", tag=tag, align_bytes=64)
-            nc.vector.tensor_tensor(ab_tile[:], b_bank, a_sb[c], MULT)
-            return ab_tile
+            second = first_product(w2_mx, words2, 1, c, "second_out")
+            ab = keep.tile([P, CHUNK // 2, PACK, 2], F32, name=f"ab{c}", tag=tag, align_bytes=ALIGN)
+            nc.vector.tensor_tensor(ab[:], second, a_of[c], MULT)
+            return ab
 
-        ab_sb = [make_ab(c, f"ab{c}") for c in range(CHUNKS - 1)]
-        g31 = keep.tile([P, H * PACK // 2], BF16, name="g31", tag="g21", align_bytes=64)
-        on_gpsimd(
-            g31[:].rearrange("p (t m j) -> p t m j", t=2, j=PACK),
-            raw3[:].rearrange("p j (m t) -> p t m j", t=PACK)[:, 2:4],
+        ab_of = [make_ab(c, f"ab{c}") for c in range(CHUNKS - 1)]
+
+        rounded3_upper = rounded_half("rounded3_1", "word_table")
+        nc.gpsimd.tensor_scalar(
+            rounded3_upper[:].rearrange("p (t m j) -> p t m j", t=PAIR, j=PACK),
+            raw3[:].rearrange("p j (m t) -> p t m j", t=PACK)[:, PAIR:PACK],
+            1.0,
+            0.0,
+            MULT,
+            ADD,
         )
-        w3_high = quantize(g31, "w31")
-        w3_low = quantize(round_first_weight(raw3, 0, on_scalar, "g30", "g30"), "w30")
-        q3 = [w3_low, w3_high]
-        ab_sb.append(make_ab(CHUNKS - 1, "g30"))
-        g4 = keep.tile([P, N * PACK], BF16, name="g4", align_bytes=64)
+        w3_upper = quantize(rounded3_upper, "w3_1")
+        rounded3_lower = rounded_half("rounded3_0", "rounded3_0")
+        round_on_scalar(rounded3_lower, raw3, 0, 0)
+        w3_mx = [quantize(rounded3_lower, "w3_0"), w3_upper]
+        ab_of.append(make_ab(CHUNKS - 1, "rounded3_0"))
+
+        rounded4 = keep.tile([P, N * PACK], BF16, name="rounded4", align_bytes=ALIGN)
         nc.scalar.copy(
-            g4[:].rearrange("p (c i j) -> p c j i", i=4, j=PACK),
-            raw4[:].rearrange("p j (c i) -> p c j i", i=4),
+            rounded4[:].rearrange("p (n e j) -> p n j e", e=4, j=PACK),
+            raw4[:].rearrange("p j (n e) -> p n j e", e=4),
         )
-        w4_codes, w4_scales = quantize(g4, "w4")
+        w4_codes, w4_scales = quantize(rounded4, "w4")
 
-        z_first = keep.tile([P, 2 * CHUNK * PACK], BF16, name="z_first", align_bytes=64)
-        z_third = keep.tile([P, CHUNK * PACK], BF16, name="z_third", align_bytes=64)
-        z_last = keep.tile([P, CHUNK * PACK], BF16, name="z_last", align_bytes=64)
-        z_of = [z_first[:, : CHUNK * PACK], z_first[:, CHUNK * PACK :], z_third[:], z_last[:]]
+        z_of = [keep.tile([P, width], BF16, name=f"z{c}", align_bytes=ALIGN) for c in range(CHUNKS)]
 
         def make_z(c):
-            c_bank = first_product(q3, x3, 2, c, "ac")
-            nc.vector.tensor_tensor(z_of[c].rearrange("p (v e t) -> p v t e", t=PACK, e=2), c_bank, ab_sb[c][:], MULT)
+            third = first_product(w3_mx, words3, 2, c, "first_third")
+            nc.vector.tensor_tensor(z_of[c][:].rearrange("p (v e t) -> p v t e", t=PACK, e=2), third, ab_of[c][:], MULT)
 
-        def second_product(z_codes, z_scales, h, target):
+        def last_product(z_codes, z_scales, h, target):
             m_cols = slice(h * P, (h + 1) * P)
             nc.tensor.matmul_mx(
                 out=target,
@@ -158,26 +172,23 @@ def tile_picked_trilin_none_p_kernel(tc, x_words, x_scales, w1, w2, w3, w4, offs
                 stop=True,
             )
 
-        def finish(first, z, split):
-            width = z.shape[1] // PACK
-            z_codes, z_scales = quantize(z, f"z{first}")
-            result = keep.tile([P, N // P, width], F32, name=f"result{first}")
-            if split:
-                for h, copy in enumerate((on_scalar, on_vector)):
-                    bank = psum.tile([P, width], F32, name=f"o{first}_{h}", tag="bo")
-                    second_product(z_codes, z_scales, h, bank[:])
+        def finish(c):
+            z_codes, z_scales = quantize(z_of[c], f"z{c}")
+            result = keep.tile([P, N // P, CHUNK], F32, name=f"result{c}")
+            if c == CHUNKS - 1:
+                for h, copy in enumerate((nc.scalar.copy, nc.vector.tensor_copy)):
+                    bank = psum.tile([P, CHUNK], F32, name=f"out{c}_{h}", tag="second_out")
+                    last_product(z_codes, z_scales, h, bank[:])
                     copy(result[:, h, :], bank[:])
             else:
-                bank = psum.tile([P, N // P, width], F32, name=f"o{first}", tag="bo")
+                bank = psum.tile([P, N // P, CHUNK], F32, name=f"out{c}", tag="second_out")
                 for h in range(N // P):
-                    second_product(z_codes, z_scales, h, bank[:, h, :])
-                on_scalar(result[:], bank[:])
-            nc.sync.dma_start(out.rearrange("(h m) v -> m h v", m=P)[:, :, first : first + width], result[:])
+                    last_product(z_codes, z_scales, h, bank[:, h, :])
+                nc.scalar.copy(result[:], bank[:])
+            nc.sync.dma_start(out.rearrange("(h m) v -> m h v", m=P)[:, :, c * CHUNK : (c + 1) * CHUNK], result[:])
 
         make_z(0)
-        make_z(1)
-        make_z(2)
-        finish(0, z_first, False)
-        make_z(3)
-        finish(2 * CHUNK, z_third, False)
-        finish(3 * CHUNK, z_last, True)
+        for c in range(1, CHUNKS):
+            make_z(c)
+            finish(c - 1)
+        finish(CHUNKS - 1)

from contextlib import ExitStack

import concourse.mybir as mybir

K, T, S, V, H, N = 512, 2048, 1536, 512, 512, 256
FLOPS = 2 * (3 * K * H * V + H * N * V)

F32 = mybir.dt.float32
BF16 = mybir.dt.bfloat16
I32 = mybir.dt.int32
U32 = mybir.dt.uint32
U16 = mybir.dt.uint16
U8 = mybir.dt.uint8
FP8X4 = mybir.dt.float8_e4m3fn_x4
MULT = mybir.AluOpType.mult
ADD = mybir.AluOpType.add

P = 128
PACK = 4
QUADRANT = 32
STRIPE = 16
CHUNK = 128
CHUNKS = V // CHUNK
PAIR = 2
ALIGN = 64


def tile_picked_trilin_none_p_kernel(tc, x_words, x_scales, w1, w2, w3, w4, offs, out):
    nc = tc.nc
    with ExitStack() as ctx:
        keep = ctx.enter_context(tc.tile_pool(name="keep", bufs=1))
        psum = ctx.enter_context(tc.psum_pool(name="psum", bufs=CHUNKS))

        offsets = keep.tile([P, S // STRIPE], U16, name="offsets")
        nc.sync.dma_start(offsets[:], offs)

        scale_table = keep.tile([P, T], U8, name="scale_table", align_bytes=ALIGN)
        nc.vector.memset(scale_table[:].bitcast(I32), 0)

        def rows_of(w):
            return w.rearrange("(p j) c -> p j c", j=PACK)

        def load_weight(w, name):
            raw = keep.tile([P, PACK, w.shape[1]], F32, name=name, tag=name, align_bytes=ALIGN)
            nc.sync.dma_start(raw[:], rows_of(w))
            return raw

        raw1 = keep.tile([P, PACK, H], F32, name="raw1", align_bytes=ALIGN)
        nc.sync.dma_start(raw1[:, 0:1, :], rows_of(w1)[:, 0:1, :])
        scale_rows = x_scales[0].bitcast(I32).rearrange("(q r) c -> r q c", r=PACK)
        for r in range(PACK):
            nc.sync.dma_start(scale_table[r:P:QUADRANT, :].bitcast(I32), scale_rows[r])
        nc.sync.dma_start(raw1[:, 1:PACK, :], rows_of(w1)[:, 1:PACK, :])
        word_table = keep.tile([P, T], U32, name="word_table", tag="word_table", align_bytes=ALIGN)
        nc.sync.dma_start(word_table[:].bitcast(I32), x_words[0].rearrange("p n j -> p (n j)").bitcast(I32))
        raw2 = []
        for side in range(2):
            raw = keep.tile([P, PACK, H // 2], F32, name=f"raw2_{side}", tag=f"raw2_{side}", align_bytes=ALIGN)
            nc.sync.dma_start(raw[:], rows_of(w2)[:, :, side * H // 2 : (side + 1) * H // 2])
            raw2.append(raw)
        raw3 = load_weight(w3, "raw3")
        raw4 = load_weight(w4, "raw4")

        def quantize(rounded, name):
            width = rounded.shape[1] // PACK
            codes = keep.tile([P, width], U32, name=name + "_codes", align_bytes=ALIGN)
            scales = keep.tile([P, width], U8, name=name + "_scales", align_bytes=ALIGN)
            nc.vector.quantize_mx(out=codes[:].bitcast(FP8X4), scales=scales[:], in_=rounded[:])
            return codes, scales

        def rounded_half(name, tag):
            return keep.tile([P, PAIR * P * PACK], BF16, name=name, tag=tag, align_bytes=ALIGN)

        def round_on_scalar(rounded, raw, half, first_m):
            count = raw.shape[2] // PACK
            nc.scalar.copy(
                rounded[:].rearrange("p (t m j) -> p m j t", t=PAIR, j=PACK)[:, first_m : first_m + count],
                raw[:].rearrange("p j (m t) -> p m j t", t=PACK)[:, :, :, PAIR * half : PAIR * (half + 1)],
            )

        def gather_words(first, count, tag):
            words = keep.tile([P, count], U32, name=f"picked_words{first}", tag=tag, align_bytes=ALIGN)
            entries = offsets[:, first // STRIPE : (first + count) // STRIPE]
            nc.vector.tensor_copy(words[:], word_table[:].indirect(entries))
            return [words[:, c * CHUNK : (c + 1) * CHUNK] for c in range(count // CHUNK)]

        def first_product(halves, words, piece, c, tag):
            bank = psum.tile([P, PACK, CHUNK], F32, name=f"product{piece}_{c}", tag=tag)
            entry = piece * V + c * CHUNK
            for t in range(PACK):
                codes, scales = halves[t // PAIR]
                m_cols = slice(t % PAIR * P, (t % PAIR + 1) * P)
                nc.tensor.matmul_mx(
                    out=bank[:, t, :],
                    lhsT=codes[:, m_cols].bitcast(FP8X4),
                    lhsT_scale=scales[:, m_cols],
                    rhs=words[c].bitcast(FP8X4),
                    rhs_scale=picked_scales[:, entry : entry + CHUNK],
                    start=True,
                    stop=True,
                )
            return bank[:].rearrange("p t (v e) -> p v t e", e=2)

        picked_scales = keep.tile([P, S], U8, name="picked_scales", align_bytes=ALIGN)
        nc.vector.tensor_copy(picked_scales[:], scale_table[:].indirect(offsets[:]))

        rounded1 = [rounded_half(f"rounded1_{half}", f"rounded1_{half}") for half in range(2)]
        for half in range(2):
            round_on_scalar(rounded1[half], raw1, half, 0)
        words1 = gather_words(0, V, "words1")
        w1_mx = [quantize(rounded1[half], f"w1_{half}") for half in range(2)]
        words_mid = gather_words(V, V + V // 2, "rounded1_1")
        rounded2 = [rounded_half(f"rounded2_{half}", f"rounded2_{half}") for half in range(2)]
        for side in range(2):
            for half in range(2):
                round_on_scalar(rounded2[half], raw2[side], half, side * P // 2)
        w2_mx = [quantize(rounded2[half], f"w2_{half}") for half in range(2)]
        words2 = words_mid[:CHUNKS]
        words3 = words_mid[CHUNKS:] + gather_words(S - V // 2, V // 2, "rounded2_1")

        width = CHUNK * PACK
        a_all = keep.tile([P, CHUNKS * width], F32, name="a_all", tag="raw2_1", align_bytes=ALIGN)
        a_of = [a_all[:, c * width : (c + 1) * width].rearrange("p (v t e) -> p v t e", t=PACK, e=2) for c in range(CHUNKS)]
        for c in range(CHUNKS):
            nc.scalar.copy(a_of[c], first_product(w1_mx, words1, 0, c, "first_third"))

        def make_ab(c, tag):
            second = first_product(w2_mx, words2, 1, c, "second_out")
            ab = keep.tile([P, CHUNK // 2, PACK, 2], F32, name=f"ab{c}", tag=tag, align_bytes=ALIGN)
            nc.vector.tensor_tensor(ab[:], second, a_of[c], MULT)
            return ab

        ab_of = [make_ab(c, f"ab{c}") for c in range(CHUNKS - 1)]

        rounded3_upper = rounded_half("rounded3_1", "word_table")
        nc.gpsimd.tensor_scalar(
            rounded3_upper[:].rearrange("p (t m j) -> p t m j", t=PAIR, j=PACK),
            raw3[:].rearrange("p j (m t) -> p t m j", t=PACK)[:, PAIR:PACK],
            1.0,
            0.0,
            MULT,
            ADD,
        )
        w3_upper = quantize(rounded3_upper, "w3_1")
        rounded3_lower = rounded_half("rounded3_0", "rounded3_0")
        round_on_scalar(rounded3_lower, raw3, 0, 0)
        w3_mx = [quantize(rounded3_lower, "w3_0"), w3_upper]
        ab_of.append(make_ab(CHUNKS - 1, "rounded3_0"))

        rounded4 = keep.tile([P, N * PACK], BF16, name="rounded4", align_bytes=ALIGN)
        nc.scalar.copy(
            rounded4[:].rearrange("p (n e j) -> p n j e", e=4, j=PACK),
            raw4[:].rearrange("p j (n e) -> p n j e", e=4),
        )
        w4_codes, w4_scales = quantize(rounded4, "w4")

        z_of = [keep.tile([P, width], BF16, name=f"z{c}", align_bytes=ALIGN) for c in range(CHUNKS)]

        def make_z(c):
            third = first_product(w3_mx, words3, 2, c, "first_third")
            nc.vector.tensor_tensor(z_of[c][:].rearrange("p (v e t) -> p v t e", t=PACK, e=2), third, ab_of[c][:], MULT)

        def last_product(z_codes, z_scales, h, target):
            m_cols = slice(h * P, (h + 1) * P)
            nc.tensor.matmul_mx(
                out=target,
                lhsT=w4_codes[:, m_cols].bitcast(FP8X4),
                lhsT_scale=w4_scales[:, m_cols],
                rhs=z_codes[:].bitcast(FP8X4),
                rhs_scale=z_scales[:],
                start=True,
                stop=True,
            )

        def finish(c):
            z_codes, z_scales = quantize(z_of[c], f"z{c}")
            result = keep.tile([P, N // P, CHUNK], F32, name=f"result{c}")
            if c == CHUNKS - 1:
                for h, copy in enumerate((nc.scalar.copy, nc.vector.tensor_copy)):
                    bank = psum.tile([P, CHUNK], F32, name=f"out{c}_{h}", tag="second_out")
                    last_product(z_codes, z_scales, h, bank[:])
                    copy(result[:, h, :], bank[:])
            else:
                bank = psum.tile([P, N // P, CHUNK], F32, name=f"out{c}", tag="second_out")
                for h in range(N // P):
                    last_product(z_codes, z_scales, h, bank[:, h, :])
                nc.scalar.copy(result[:], bank[:])
            nc.sync.dma_start(out.rearrange("(h m) v -> m h v", m=P)[:, :, c * CHUNK : (c + 1) * CHUNK], result[:])

        make_z(0)
        for c in range(1, CHUNKS):
            make_z(c)
            finish(c - 1)
        finish(CHUNKS - 1)
